import numpy as np
import ml_dtypes


def mxq(x, axis, fmt="e4m3"):
    dtype, down = {"e4m3": (ml_dtypes.float8_e4m3fn, 7), "e5m2": (ml_dtypes.float8_e5m2, 14)}[fmt]
    v = np.moveaxis(np.asarray(x, np.float32).astype(ml_dtypes.bfloat16).astype(np.float64), axis, -1)
    blocks = v.reshape(v.shape[:-1] + (-1, 32))
    amax = np.abs(blocks).max(-1, keepdims=True)
    byte = np.maximum(np.where(amax > 0, np.frexp(amax)[1] - 1 + 127, 0) - down, 1)
    scale = np.exp2(byte - 127.0)
    codes = (blocks / scale).astype(np.float32).astype(dtype).astype(np.float64)
    return np.moveaxis((codes * scale).reshape(v.shape), -1, axis)


WIDE = False


def mx_kscale(k):
    if not WIDE:
        return np.ones(k)
    levels = np.array([10, -10, 5, -5, 0])
    if k % 512:
        return np.exp2(np.random.permutation(np.resize(levels, k // 32))).repeat(32)
    a = np.empty((k // 512, 16))
    for p in range(k // 512):
        a[p, :8] = np.random.permutation(np.resize(levels, 8))
        for g in range(8):
            far = levels[np.abs(levels - a[p, g]) >= 10]
            a[p, g + 8] = far[np.random.randint(len(far))]
    return np.exp2(a.ravel()).repeat(32)


def f64(x):
    return np.asarray(x).astype(np.float64)


def striped(idx):
    return np.tile(idx.reshape(-1, 16).T, (8, 1)).astype(np.uint16)


def unstriped(offs):
    return offs[:16].T.reshape(-1).astype(np.int64)


def pack_weight(w):
    k, n = w.shape
    w = f64(np.asarray(w, np.float32).astype(ml_dtypes.bfloat16)).reshape(k // 32, 32, n)
    amax = np.abs(w).max(1)
    byte = np.clip(np.where(amax > 0, np.frexp(amax)[1] - 1 + 127 - 7, 1), 1, 254)
    scaled = (w * np.exp2(127.0 - byte)[:, None, :]).reshape(k, n).astype(np.float32)
    words = np.ascontiguousarray(scaled.reshape(k // 512, 128, 4, n).transpose(0, 1, 3, 2)).astype(ml_dtypes.float8_e4m3fn).view(np.uint8)
    return words, np.ascontiguousarray(byte.astype(np.uint8).reshape(k // 512, 16, n))


def unpack_weight(words, scales):
    g, p, n, _ = words.shape
    vals = np.ascontiguousarray(words).view(ml_dtypes.float8_e4m3fn).astype(np.float64) * np.repeat(np.exp2(scales.astype(np.float64) - 127.0), 8, axis=1)[..., None]
    return vals.transpose(0, 1, 3, 2).reshape(g * 512, n)


K, T, S, D, N = 512, 2048, 1024, 4, 256
P = 2 ** 7


def setup_inputs():
    n = np.random.standard_normal
    s = mx_kscale(K)[:, None]
    packed_xT = pack_weight(n((K, T)) * s)
    return {
        "x_words": packed_xT[0],
        "x_scales": packed_xT[1],
        "w1": (n((K, N)) / np.sqrt(K) / s).astype(np.float32),
        "w2": (n((K, N)) / np.sqrt(K) / s).astype(np.float32),
        "te": (np.tile(np.random.uniform(0.1, 1.5, S), (P, 1))).astype(np.float32),
        "sig": (np.random.uniform(0.1, 1.5, (N, S))).astype(np.float32),
        "offs": striped(np.random.permutation(T)[:S]),
    }


def reference(x_words, x_scales, w1, w2, te, sig, offs):
    xq = unpack_weight(x_words, x_scales)[:, unstriped(offs)]
    ya = mxq(f64(w1), 0, "e4m3").T @ xq
    sa = np.log(np.exp(ya) + 1.0)
    amp = sa.reshape(len(sa), -1, D).mean(axis=2) + 0.3
    yr = mxq(f64(w2), 0, "e4m3").T @ xq
    sr = np.log(np.exp(yr) + 1.0)
    rel = sr.reshape(len(sr), -1, D).mean(axis=2)
    dec = np.exp(-1.0 * (np.repeat(rel, D, axis=1) * f64(te)[:1]))
    jr = (-1.0 * (f64(te)[:1] * dec)) * np.repeat(amp, D, axis=1)
    hrr0 = (jr) ** 2
    hrr = hrr0.reshape(len(hrr0), -1, D).sum(axis=2)
    res = f64(sig) - (np.repeat(amp, D, axis=1) * dec)
    ga0 = dec * res
    ga = ga0.reshape(len(ga0), -1, D).sum(axis=2)
    har0 = dec * jr
    har = har0.reshape(len(har0), -1, D).sum(axis=2)
    gr0 = jr * res
    gr = gr0.reshape(len(gr0), -1, D).sum(axis=2)
    haa0 = (dec) ** 2
    haa = haa0.reshape(len(haa0), -1, D).sum(axis=2)
    det = (haa + 0.1) * (hrr + 0.3) - ((har) ** 2)
    return amp + ((hrr + 0.3) * ga - (har * gr)) / det

@@ -1,0 +1,298 @@
+import math
+from contextlib import ExitStack
+
+import concourse.mybir as mybir
+from concourse.masks import make_identity
+
+K, T, S, D, N = 512, 2048, 1024, 4, 256
+V = S // D
+FLOPS = 2 * 2 * K * N * S
+
+F32 = mybir.dt.float32
+BF16 = mybir.dt.bfloat16
+I32 = mybir.dt.int32
+U32 = mybir.dt.uint32
+U16 = mybir.dt.uint16
+U8 = mybir.dt.uint8
+FP8X4 = mybir.dt.float8_e4m3fn_x4
+ACT = mybir.ActivationFunctionType
+ALU = mybir.AluOpType
+
+P = 128
+PACK = 4
+VB = V // P
+MB = N // P
+KNEE = 11.0
+RATE, AMP = 0, 1
+FIT_SCALE = 10.0 * D
+
+
+def tile_picked_amp_p_kernel(tc, x_words, x_scales, w1, w2, te, sig, offs, out):
+    nc = tc.nc
+    with ExitStack() as ctx:
+        keep = ctx.enter_context(tc.tile_pool(name="keep", bufs=1))
+        psum = ctx.enter_context(tc.psum_pool(name="psum", bufs=1))
+
+        def sb(name, shape, dtype=F32, tag=None):
+            return keep.tile(shape, dtype, name=name, tag=tag or name, align_bytes=64)
+
+        offsets = keep.tile([P, S // 16], U16, name="offsets")
+        bank = [psum.tile([P, 512], F32, name="bank%d" % b) for b in range(8)]
+
+        words_all = sb("words_all", [P, T], U32)
+        scales_all = sb("scales_all", [P, T], U8)
+        w_raw = [sb("w_raw%d" % i, [P, PACK, N]) for i in range(2)]
+        t_col = sb("t_col", [P, VB, D])
+        sig_sb = [sb("sig%d" % mb, [P, S]) for mb in range(MB)]
+
+        nc.vector.memset(scales_all[:].bitcast(I32), 0)
+        nc.sync.dma_start(offsets[:], offs)
+        nc.sync.dma_start(out=words_all[:].bitcast(I32), in_=x_words[0].rearrange("p c r -> p (c r)").bitcast(I32))
+        for q in range(4):
+            nc.sync.dma_start(out=scales_all[32 * q : 32 * q + 4, :].bitcast(I32), in_=x_scales[0, 4 * q : 4 * q + 4, :].bitcast(I32))
+        for i, w in enumerate((w2, w1)):
+            nc.sync.dma_start(out=w_raw[i][:], in_=w.rearrange("(p j) n -> p j n", j=PACK))
+        nc.sync.dma_start(out=t_col[:], in_=te[0, :].rearrange("(b v d) -> v b d", b=VB, d=D))
+        for mb in range(MB):
+            nc.sync.dma_start(out=sig_sb[mb][:], in_=sig[mb * P : (mb + 1) * P, :])
+
+        knee = sb("knee", [P, 1])
+        floor = sb("floor", [P, 1])
+        nc.vector.memset(knee[:], KNEE)
+        nc.scalar.activation(floor[:], knee[:], ACT.Sigmoid, scale=-1.0)
+        ident = sb("ident", [P, P])
+        make_identity(nc, ident[:])
+        rate_scale = sb("rate_scale", [P, VB, D])
+        nc.gpsimd.tensor_scalar(rate_scale[:], t_col[:], -1.0 / D, 0.0, ALU.mult, ALU.add)
+
+        w_codes = [sb("w_codes%d" % i, [P, N], U32) for i in range(2)]
+        w_bytes = [sb("w_bytes%d" % i, [P, N], U8) for i in range(2)]
+        x_codes, x_bytes = {}, {}
+
+        def quantize(i):
+            grouped = sb("w_grouped%d" % i, [P, N, PACK], BF16)
+            nc.scalar.copy(grouped[:], w_raw[i][:].rearrange("p j n -> p n j"))
+            nc.vector.quantize_mx(out=w_codes[i][:].bitcast(FP8X4), scales=w_bytes[i][:], in_=grouped[:].rearrange("p n j -> p (n j)"))
+
+        def gather(table, vb, dst):
+            picks = offsets[:, vb * P * D // 16 : (vb + 1) * P * D // 16]
+            nc.vector.tensor_copy(dst[:].rearrange("p (d v) -> p v d", d=D), table[:].indirect(picks))
+
+        x_codes[0] = sb("x_codes0", [P, D * P], U32)
+        gather(words_all, 0, x_codes[0])
+        x_bytes[0] = sb("x_bytes0", [P, D * P], U8)
+        gather(scales_all, 0, x_bytes[0])
+        x_codes[1] = sb("x_codes1", [P, D * P], U32)
+        gather(words_all, 1, x_codes[1])
+        quantize(RATE)
+        x_bytes[1] = sb("x_bytes1", [P, D * P], U8, tag="w_grouped0")
+        gather(scales_all, 1, x_bytes[1])
+        quantize(AMP)
+
+        def product(i, vb, d, dst):
+            cols = slice(d * P, (d + 1) * P)
+            nc.tensor.matmul_mx(
+                out=dst,
+                lhsT=x_codes[vb][:, cols].bitcast(FP8X4),
+                lhsT_scale=x_bytes[vb][:, cols],
+                rhs=w_codes[i][:].bitcast(FP8X4),
+                rhs_scale=w_bytes[i][:],
+                start=True,
+                stop=True,
+            )
+
+        def rate_y(vb, d):
+            return bank[2 * vb + d // 2][:, (d % 2) * N : (d % 2 + 1) * N]
+
+        for vb in range(VB):
+            for d in range(D):
+                product(RATE, vb, d, rate_y(vb, d))
+        for d in range(D):
+            for vb in range(VB):
+                product(AMP, vb, d, bank[D + d][:, vb * N : (vb + 1) * N])
+
+        sigm_first = sb("sigm_first", [P, 2, 2 * N], tag="w_raw1")
+        sigm = [[sb("sigm%d_%d" % (i, b), [P, 2 * N])[:] if i or b > 1 else sigm_first[:, b, :] for b in range(D)] for i in range(2)]
+        prod = [[sb("prod%d_%d" % (i, d), [P, VB * N]) for d in range(D)] for i in range(2)]
+        over = [[sb("over%d_%d" % (i, d), [P, VB * N]) for d in range(D)] for i in range(2)]
+        log_prod = [sb("log_prod%d" % i, [P, VB * N]) for i in range(2)]
+        amp4 = sb("amp4", [P, VB * N])
+        rate4 = sb("rate4", [P, VB * N])
+        amp_sq = sb("amp_sq", [P, VB * N])
+        amp_quad = sb("amp_quad", [P, VB * N])
+        damp = rate4
+
+        blocks = [slice(vb * N, (vb + 1) * N) for vb in range(VB)]
+        whole = slice(0, VB * N)
+
+        def prod_step(i, d, cols, s):
+            if d == 0:
+                nc.vector.tensor_scalar(prod[i][0][:, cols], s, floor[:], None, ALU.max)
+            else:
+                nc.vector.scalar_tensor_tensor(prod[i][d][:, cols], s, floor[:], prod[i][d - 1][:, cols], ALU.max, ALU.mult)
+
+        def over_step(i, d, cols, y):
+            if d == 0:
+                nc.vector.tensor_scalar(over[i][0][:, cols], y, KNEE, -D * KNEE, ALU.max, ALU.add)
+            else:
+                nc.vector.scalar_tensor_tensor(over[i][d][:, cols], y, KNEE, over[i][d - 1][:, cols], ALU.max, ALU.add)
+
+        for i in range(2):
+            for b in range(D):
+                nc.scalar.activation(sigm[i][b], bank[D * i + b][:], ACT.Sigmoid, scale=-1.0)
+
+        def rate_prod(vb, d):
+            prod_step(RATE, d, blocks[vb], sigm[RATE][2 * vb + d // 2][:, (d % 2) * N : (d % 2 + 1) * N])
+
+        def rate_over(vb, d):
+            over_step(RATE, d, blocks[vb], rate_y(vb, d))
+
+        def rate_total(vb):
+            nc.vector.tensor_tensor(rate4[:, blocks[vb]], over[RATE][D - 1][:, blocks[vb]], log_prod[RATE][:, blocks[vb]], ALU.subtract)
+
+        for d in range(D):
+            rate_prod(0, d)
+            rate_over(0, d)
+        for d in range(D):
+            rate_prod(1, d)
+            prod_step(AMP, d, whole, sigm[AMP][d])
+        nc.scalar.activation(log_prod[RATE][:], prod[RATE][D - 1][:], ACT.Ln)
+        nc.scalar.activation(log_prod[AMP][:], prod[AMP][D - 1][:], ACT.Ln)
+        rate_total(0)
+        for d in range(D):
+            rate_over(1, d)
+            over_step(AMP, d, whole, bank[D + d][:])
+        rate_total(1)
+        nc.vector.scalar_tensor_tensor(amp4[:], over[AMP][D - 1][:], 0.3 * D, log_prod[AMP][:], ALU.add, ALU.subtract)
+
+        for vb in range(VB):
+            for d in range(D):
+                for mb in range(MB):
+                    c0 = (d % 2) * N + mb * P
+                    j0 = vb * P * D + d
+                    nc.tensor.transpose(bank[2 * vb + d // 2][:, c0 : c0 + P], sig_sb[mb][:, j0 : (vb + 1) * P * D : D], ident[:])
+
+        def turn(dst, col0, srcs):
+            for mb in range(MB):
+                for n, src in enumerate(srcs):
+                    nc.tensor.matmul(
+                        dst[:, col0 + mb * P : col0 + (mb + 1) * P],
+                        src(mb),
+                        ident[:],
+                        start=(n == 0),
+                        stop=(n == len(srcs) - 1),
+                        is_transpose=True,
+                    )
+
+        def cols_of(ap):
+            return lambda mb: ap[:, mb * P : (mb + 1) * P]
+
+        q_bank = [bank[4], bank[6]]
+        h_bank = [bank[5], bank[7]]
+        p_bank = [bank[0], bank[2]]
+        u_bank = [bank[1], bank[3]]
+
+        def per_block(name, shape):
+            return [sb("%s%d" % (name, vb), shape) for vb in range(VB)]
+
+        dec = per_block("dec", [P, D, N])
+        dec_sq = per_block("dec_sq", [P, D, N])
+        dec_sig = per_block("dec_sig", [P, D, N])
+        slope_sq = per_block("slope_sq", [P, D, N])
+        q1 = per_block("q1_", [P, D, N])
+        p1 = per_block("p1_", [P, D, N])
+        q1_sq = per_block("q1_sq", [P, N])
+        q1_p1 = per_block("q1_p1", [P, N])
+        hrr = per_block("hrr", [P, N])
+        det_lead = per_block("det_lead", [P, N])
+        det = per_block("det", [P, N])
+        num_lead = per_block("num_lead", [P, N])
+        num = per_block("num", [P, N])
+        root = per_block("root", [P, N])
+        inv = per_block("inv", [P, N])
+        res = per_block("res", [P, N])
+
+        def decays(vb):
+            for d in range(D):
+                nc.scalar.activation(dec[vb][:, d, :], rate4[:, blocks[vb]], ACT.Exp, scale=rate_scale[:, vb, d : d + 1])
+
+        def squares(vb, halves=(0, 1)):
+            for h in halves:
+                nc.scalar.activation(dec_sq[vb][:, 2 * h : 2 * h + 2, :], dec[vb][:, 2 * h : 2 * h + 2, :], ACT.Square)
+
+        def slopes(vb):
+            for d in range(D):
+                nc.scalar.activation(slope_sq[vb][:, d, :], dec[vb][:, d, :], ACT.Square, scale=t_col[:, vb, d : d + 1])
+
+        def timed_step(acc, src, vb, d):
+            t_d = t_col[:, vb, d : d + 1]
+            if d == 0:
+                nc.vector.tensor_scalar(acc[:, 0, :], src[:, 0, :], t_d, None, ALU.mult)
+            else:
+                nc.vector.scalar_tensor_tensor(acc[:, d, :], src[:, d, :], t_d, acc[:, d - 1, :], ALU.mult, ALU.add)
+
+        def weigh(vb, h):
+            nc.vector.scalar_tensor_tensor(
+                dec_sig[vb][:, 2 * h : 2 * h + 2, :],
+                dec[vb][:, 2 * h : 2 * h + 2, :],
+                FIT_SCALE,
+                bank[2 * vb + h][:].rearrange("p (d m) -> p d m", d=2),
+                ALU.mult,
+                ALU.mult,
+            )
+
+        def turn_fit(vb):
+            turn(p_bank[vb], 0, [cols_of(dec_sig[vb][:, d, :]) for d in range(D)] + [cols_of(amp4[:, blocks[vb]])])
+
+        def turn_q0(vb):
+            turn(q_bank[vb], 0, [cols_of(dec_sq[vb][:, d, :]) for d in range(D)])
+
+        def turn_h(vb):
+            turn(h_bank[vb], 0, [cols_of(slope_sq[vb][:, d, :]) for d in range(D)] + [cols_of(damp[:, blocks[vb]])])
+            nc.scalar.copy(hrr[vb][:], h_bank[vb][:, 0:N])
+
+        def cross(vb):
+            nc.vector.tensor_tensor(q1_sq[vb][:], q1[vb][:, D - 1, :], q1[vb][:, D - 1, :], ALU.mult)
+            nc.vector.tensor_tensor(q1_p1[vb][:], q1[vb][:, D - 1, :], p1[vb][:, D - 1, :], ALU.mult)
+            turn(q_bank[vb], N, [cols_of(q1_sq[vb][:])])
+            turn(u_bank[vb], 0, [cols_of(q1_p1[vb][:])])
+
+        def solve(vb):
+            nc.vector.scalar_tensor_tensor(det_lead[vb][:], q_bank[vb][:, 0:N], 0.1, hrr[vb][:], ALU.add, ALU.mult)
+            nc.vector.tensor_tensor(num_lead[vb][:], hrr[vb][:], p_bank[vb][:, 0:N], ALU.mult)
+            nc.vector.tensor_tensor(det[vb][:], det_lead[vb][:], q_bank[vb][:, N : 2 * N], ALU.subtract)
+            nc.scalar.activation(root[vb][:], det[vb][:], ACT.Abs_reciprocal_sqrt)
+            nc.scalar.activation(inv[vb][:], root[vb][:], ACT.Square)
+            nc.vector.tensor_tensor(num[vb][:], num_lead[vb][:], u_bank[vb][:, 0:N], ALU.subtract)
+
+        def finish(vb):
+            nc.vector.scalar_tensor_tensor(res[vb][:], num[vb][:], 1.0 / FIT_SCALE, inv[vb][:], ALU.mult, ALU.mult)
+            nc.sync.dma_start(
+                out=out.rearrange("(b p) v -> p b v", p=P)[:, :, vb * P : (vb + 1) * P],
+                in_=res[vb][:].rearrange("p (b v) -> p b v", b=MB),
+            )
+
+        decays(0)
+        decays(1)
+        squares(0)
+        nc.scalar.activation(amp_sq[:], amp4[:], ACT.Square, scale=1.0 / D)
+        nc.scalar.activation(amp_quad[:], amp_sq[:], ACT.Square)
+        nc.scalar.activation(damp[:], amp_quad[:], ACT.Abs_reciprocal_sqrt, scale=1.0 / (0.3 * 0.3))
+        slopes(0)
+        squares(1, (1,))
+        slopes(1)
+        for vb in range(VB):
+            weigh(vb, 0)
+            if vb == 1:
+                nc.vector.tensor_tensor(dec_sq[vb][:, 0 : 2, :], dec[vb][:, 0 : 2, :], dec[vb][:, 0 : 2, :], ALU.mult)
+            weigh(vb, 1)
+            for d in range(D):
+                timed_step(p1[vb], dec_sig[vb], vb, d)
+                timed_step(q1[vb], dec_sq[vb], vb, d)
+            turn_q0(vb)
+            turn_fit(vb)
+            turn_h(vb)
+            cross(vb)
+        for vb in range(VB):
+            solve(vb)
+            finish(vb)

@@ -65,6 +65,9 @@ def tile_picked_amp_p_kernel(tc, x_words, x_scales, w1, w2, te, sig, offs, out):
         rate_scale = sb("rate_scale", [P, VB, D])
         nc.gpsimd.tensor_scalar(rate_scale[:], t_col[:], -1.0 / D, 0.0, ALU.mult, ALU.add)
 
+        rate_bias = sb("rate_bias", [P, VB, D])
+        nc.gpsimd.tensor_scalar(rate_bias[:], t_col[:], KNEE, 0.0, ALU.mult, ALU.add)
+
         w_codes = [sb("w_codes%d" % i, [P, N], U32) for i in range(2)]
         w_bytes = [sb("w_bytes%d" % i, [P, N], U8) for i in range(2)]
         x_codes, x_bytes = {}, {}
@@ -111,13 +114,16 @@ def tile_picked_amp_p_kernel(tc, x_words, x_scales, w1, w2, te, sig, offs, out):
             for vb in range(VB):
                 product(AMP, vb, d, bank[D + d][:, vb * N : (vb + 1) * N])
 
-        sigm_first = sb("sigm_first", [P, 2, 2 * N], tag="w_raw1")
-        sigm = [[sb("sigm%d_%d" % (i, b), [P, 2 * N])[:] if i or b > 1 else sigm_first[:, b, :] for b in range(D)] for i in range(2)]
-        prod = [[sb("prod%d_%d" % (i, d), [P, VB * N]) for d in range(D)] for i in range(2)]
+        sigm_rate = sb("sigm_rate", [P, D, 2 * N], tag="w_raw1")
+        sigm = [[sigm_rate[:, b, :] for b in range(D)], [sb("sigm_amp%d" % b, [P, 2 * N])[:] for b in range(D)]]
+        prod_last = sb("prod_last", [P, 2, VB * N], tag="dec0")
+        prod = [[sb("prod%d_%d" % (i, d), [P, VB * N]) for d in range(D - 1)] + [prod_last[:, 1 - i, :]] for i in range(2)]
         over = [[sb("over%d_%d" % (i, d), [P, VB * N]) for d in range(D)] for i in range(2)]
-        log_prod = [sb("log_prod%d" % i, [P, VB * N]) for i in range(2)]
-        amp4 = sb("amp4", [P, VB * N])
+        log_prod = [sigm[AMP][0], sb("log_prod_amp", [P, VB * N])]
+        amp4 = over[AMP][D - 1]
         rate4 = sb("rate4", [P, VB * N])
+        over[RATE][D - 1] = rate4
+        rate_over0 = sb("rate_over0", [P, N])
         amp_sq = sb("amp_sq", [P, VB * N])
         amp_quad = sb("amp_quad", [P, VB * N])
         damp = rate4
@@ -131,11 +137,13 @@ def tile_picked_amp_p_kernel(tc, x_words, x_scales, w1, w2, te, sig, offs, out):
             else:
                 nc.vector.scalar_tensor_tensor(prod[i][d][:, cols], s, floor[:], prod[i][d - 1][:, cols], ALU.max, ALU.mult)
 
-        def over_step(i, d, cols, y):
-            if d == 0:
-                nc.vector.tensor_scalar(over[i][0][:, cols], y, KNEE, -D * KNEE, ALU.max, ALU.add)
-            else:
+        def over_step(i, d, cols, y, seed=None):
+            if d > 0:
                 nc.vector.scalar_tensor_tensor(over[i][d][:, cols], y, KNEE, over[i][d - 1][:, cols], ALU.max, ALU.add)
+            elif seed is None:
+                nc.vector.tensor_scalar(over[i][0][:, cols], y, KNEE, None, ALU.max)
+            else:
+                nc.vector.scalar_tensor_tensor(over[i][0][:, cols], y, KNEE, seed[:, cols], ALU.max, ALU.subtract)
 
         for i in range(2):
             for b in range(D):
@@ -145,10 +153,16 @@ def tile_picked_amp_p_kernel(tc, x_words, x_scales, w1, w2, te, sig, offs, out):
             prod_step(RATE, d, blocks[vb], sigm[RATE][2 * vb + d // 2][:, (d % 2) * N : (d % 2 + 1) * N])
 
         def rate_over(vb, d):
-            over_step(RATE, d, blocks[vb], rate_y(vb, d))
+            if (vb, d) == (0, D - 1):
+                nc.vector.scalar_tensor_tensor(rate_over0[:], rate_y(0, d), KNEE, over[RATE][d - 1][:, blocks[0]], ALU.max, ALU.add)
+            else:
+                over_step(RATE, d, blocks[vb], rate_y(vb, d), log_prod[RATE] if vb else None)
+
+        def rate_log(vb):
+            nc.scalar.activation(log_prod[RATE][:, blocks[vb]], prod[RATE][D - 1][:, blocks[vb]], ACT.Ln)
 
         def rate_total(vb):
-            nc.vector.tensor_tensor(rate4[:, blocks[vb]], over[RATE][D - 1][:, blocks[vb]], log_prod[RATE][:, blocks[vb]], ALU.subtract)
+            nc.vector.tensor_tensor(rate4[:, blocks[vb]], rate_over0[:], log_prod[RATE][:, blocks[vb]], ALU.subtract)
 
         for d in range(D):
             rate_prod(0, d)
@@ -156,14 +170,14 @@ def tile_picked_amp_p_kernel(tc, x_words, x_scales, w1, w2, te, sig, offs, out):
         for d in range(D):
             rate_prod(1, d)
             prod_step(AMP, d, whole, sigm[AMP][d])
-        nc.scalar.activation(log_prod[RATE][:], prod[RATE][D - 1][:], ACT.Ln)
+            if d == 0:
+                rate_log(0)
+                rate_total(0)
+        rate_log(1)
         nc.scalar.activation(log_prod[AMP][:], prod[AMP][D - 1][:], ACT.Ln)
-        rate_total(0)
         for d in range(D):
             rate_over(1, d)
-            over_step(AMP, d, whole, bank[D + d][:])
-        rate_total(1)
-        nc.vector.scalar_tensor_tensor(amp4[:], over[AMP][D - 1][:], 0.3 * D, log_prod[AMP][:], ALU.add, ALU.subtract)
+            over_step(AMP, d, whole, bank[D + d][:], log_prod[AMP])
 
         for vb in range(VB):
             for d in range(D):
@@ -173,14 +187,14 @@ def tile_picked_amp_p_kernel(tc, x_words, x_scales, w1, w2, te, sig, offs, out):
                     nc.tensor.transpose(bank[2 * vb + d // 2][:, c0 : c0 + P], sig_sb[mb][:, j0 : (vb + 1) * P * D : D], ident[:])
 
         def turn(dst, col0, srcs):
-            for mb in range(MB):
-                for n, src in enumerate(srcs):
+            for n, src in enumerate(srcs):
+                for mb in range(MB):
                     nc.tensor.matmul(
                         dst[:, col0 + mb * P : col0 + (mb + 1) * P],
                         src(mb),
                         ident[:],
-                        start=(n == 0),
-                        stop=(n == len(srcs) - 1),
+                        start=(n == 0 and mb == 0),
+                        stop=(n == len(srcs) - 1 and mb == MB - 1),
                         is_transpose=True,
                     )
 
@@ -214,7 +228,7 @@ def tile_picked_amp_p_kernel(tc, x_words, x_scales, w1, w2, te, sig, offs, out):
 
         def decays(vb):
             for d in range(D):
-                nc.scalar.activation(dec[vb][:, d, :], rate4[:, blocks[vb]], ACT.Exp, scale=rate_scale[:, vb, d : d + 1])
+                nc.scalar.activation(dec[vb][:, d, :], rate4[:, blocks[vb]], ACT.Exp, scale=rate_scale[:, vb, d : d + 1], bias=rate_bias[:, vb, d : d + 1])
 
         def squares(vb, halves=(0, 1)):
             for h in halves:
@@ -257,12 +271,18 @@ def tile_picked_amp_p_kernel(tc, x_words, x_scales, w1, w2, te, sig, offs, out):
             turn(q_bank[vb], N, [cols_of(q1_sq[vb][:])])
             turn(u_bank[vb], 0, [cols_of(q1_p1[vb][:])])
 
-        def solve(vb):
+        def det_first(vb):
             nc.vector.scalar_tensor_tensor(det_lead[vb][:], q_bank[vb][:, 0:N], 0.1, hrr[vb][:], ALU.add, ALU.mult)
-            nc.vector.tensor_tensor(num_lead[vb][:], hrr[vb][:], p_bank[vb][:, 0:N], ALU.mult)
+
+        def num_first(vb):
+            nc.vector.scalar_tensor_tensor(num_lead[vb][:], p_bank[vb][:, 0:N], D * (0.3 - KNEE), hrr[vb][:], ALU.add, ALU.mult)
+
+        def det_second(vb):
             nc.vector.tensor_tensor(det[vb][:], det_lead[vb][:], q_bank[vb][:, N : 2 * N], ALU.subtract)
             nc.scalar.activation(root[vb][:], det[vb][:], ACT.Abs_reciprocal_sqrt)
             nc.scalar.activation(inv[vb][:], root[vb][:], ACT.Square)
+
+        def num_second(vb):
             nc.vector.tensor_tensor(num[vb][:], num_lead[vb][:], u_bank[vb][:, 0:N], ALU.subtract)
 
         def finish(vb):
@@ -273,18 +293,18 @@ def tile_picked_amp_p_kernel(tc, x_words, x_scales, w1, w2, te, sig, offs, out):
             )
 
         decays(0)
+        for h in range(2):
+            pair = dec[0][:, 2 * h : 2 * h + 2, :]
+            nc.gpsimd.tensor_tensor(dec_sq[0][:, 2 * h : 2 * h + 2, :], pair, pair, ALU.mult)
         decays(1)
-        squares(0)
-        nc.scalar.activation(amp_sq[:], amp4[:], ACT.Square, scale=1.0 / D)
+        slopes(0)
+        nc.scalar.activation(amp_sq[:], amp4[:], ACT.Square, scale=1.0 / D, bias=0.3 - KNEE)
         nc.scalar.activation(amp_quad[:], amp_sq[:], ACT.Square)
         nc.scalar.activation(damp[:], amp_quad[:], ACT.Abs_reciprocal_sqrt, scale=1.0 / (0.3 * 0.3))
-        slopes(0)
-        squares(1, (1,))
+        squares(1)
         slopes(1)
         for vb in range(VB):
             weigh(vb, 0)
-            if vb == 1:
-                nc.vector.tensor_tensor(dec_sq[vb][:, 0 : 2, :], dec[vb][:, 0 : 2, :], dec[vb][:, 0 : 2, :], ALU.mult)
             weigh(vb, 1)
             for d in range(D):
                 timed_step(p1[vb], dec_sig[vb], vb, d)
@@ -293,6 +313,6 @@ def tile_picked_amp_p_kernel(tc, x_words, x_scales, w1, w2, te, sig, offs, out):
             turn_fit(vb)
             turn_h(vb)
             cross(vb)
-        for vb in range(VB):
-            solve(vb)
-            finish(vb)
+        for step in (det_first, det_second, num_first, num_second, finish):
+            for vb in range(VB):
+                step(vb)

@@ -68,6 +68,9 @@ def tile_picked_amp_p_kernel(tc, x_words, x_scales, w1, w2, te, sig, offs, out):
         rate_bias = sb("rate_bias", [P, VB, D])
         nc.gpsimd.tensor_scalar(rate_bias[:], t_col[:], KNEE, 0.0, ALU.mult, ALU.add)
 
+        t_sq = sb("t_sq", [P, VB, D])
+        nc.gpsimd.tensor_tensor(t_sq[:], t_col[:], t_col[:], ALU.mult)
+
         w_codes = [sb("w_codes%d" % i, [P, N], U32) for i in range(2)]
         w_bytes = [sb("w_bytes%d" % i, [P, N], U8) for i in range(2)]
         x_codes, x_bytes = {}, {}
@@ -235,11 +238,11 @@ def tile_picked_amp_p_kernel(tc, x_words, x_scales, w1, w2, te, sig, offs, out):
                 nc.scalar.activation(dec_sq[vb][:, 2 * h : 2 * h + 2, :], dec[vb][:, 2 * h : 2 * h + 2, :], ACT.Square)
 
         def slopes(vb):
-            for d in range(D):
+            for d in range(0 if vb in (1,) else D):
                 nc.scalar.activation(slope_sq[vb][:, d, :], dec[vb][:, d, :], ACT.Square, scale=t_col[:, vb, d : d + 1])
 
-        def timed_step(acc, src, vb, d):
-            t_d = t_col[:, vb, d : d + 1]
+        def timed_step(acc, src, vb, d, col=t_col):
+            t_d = col[:, vb, d : d + 1]
             if d == 0:
                 nc.vector.tensor_scalar(acc[:, 0, :], src[:, 0, :], t_d, None, ALU.mult)
             else:
@@ -256,17 +259,20 @@ def tile_picked_amp_p_kernel(tc, x_words, x_scales, w1, w2, te, sig, offs, out):
             )
 
         def turn_fit(vb):
-            turn(p_bank[vb], 0, [cols_of(dec_sig[vb][:, d, :]) for d in range(D)] + [cols_of(amp4[:, blocks[vb]])])
+            pairs = sb("pairs%d" % vb, [P, 2, N])
+            if vb in (1,):
+                nc.vector.tensor_tensor(pairs[:], dec_sig[vb][:, 0:2, :], dec_sig[vb][:, 2:4, :], ALU.add)
+            turn(p_bank[vb], 0, [cols_of((pairs if vb in (1,) else dec_sig[vb])[:, d, :]) for d in range(2 if vb in (1,) else D)] + [cols_of(amp4[:, blocks[vb]])])
 
         def turn_q0(vb):
             turn(q_bank[vb], 0, [cols_of(dec_sq[vb][:, d, :]) for d in range(D)])
 
         def turn_h(vb):
-            turn(h_bank[vb], 0, [cols_of(slope_sq[vb][:, d, :]) for d in range(D)] + [cols_of(damp[:, blocks[vb]])])
+            turn(h_bank[vb], 0, [cols_of(slope_sq[vb][:, d, :]) for d in range(D - 1 if vb in (1,) else 0, D)] + [cols_of(damp[:, blocks[vb]])])
             nc.scalar.copy(hrr[vb][:], h_bank[vb][:, 0:N])
 
         def cross(vb):
-            nc.vector.tensor_tensor(q1_sq[vb][:], q1[vb][:, D - 1, :], q1[vb][:, D - 1, :], ALU.mult)
+            nc.scalar.activation(q1_sq[vb][:], q1[vb][:, D - 1, :], ACT.Square)
             nc.vector.tensor_tensor(q1_p1[vb][:], q1[vb][:, D - 1, :], p1[vb][:, D - 1, :], ALU.mult)
             turn(q_bank[vb], N, [cols_of(q1_sq[vb][:])])
             turn(u_bank[vb], 0, [cols_of(q1_p1[vb][:])])
@@ -297,11 +303,11 @@ def tile_picked_amp_p_kernel(tc, x_words, x_scales, w1, w2, te, sig, offs, out):
             pair = dec[0][:, 2 * h : 2 * h + 2, :]
             nc.gpsimd.tensor_tensor(dec_sq[0][:, 2 * h : 2 * h + 2, :], pair, pair, ALU.mult)
         decays(1)
-        slopes(0)
+        squares(1)
         nc.scalar.activation(amp_sq[:], amp4[:], ACT.Square, scale=1.0 / D, bias=0.3 - KNEE)
         nc.scalar.activation(amp_quad[:], amp_sq[:], ACT.Square)
         nc.scalar.activation(damp[:], amp_quad[:], ACT.Abs_reciprocal_sqrt, scale=1.0 / (0.3 * 0.3))
-        squares(1)
+        slopes(0)
         slopes(1)
         for vb in range(VB):
             weigh(vb, 0)
@@ -309,6 +315,8 @@ def tile_picked_amp_p_kernel(tc, x_words, x_scales, w1, w2, te, sig, offs, out):
             for d in range(D):
                 timed_step(p1[vb], dec_sig[vb], vb, d)
                 timed_step(q1[vb], dec_sq[vb], vb, d)
+                if vb in (1,):
+                    timed_step(slope_sq[vb], dec_sq[vb], vb, d, t_sq)
             turn_q0(vb)
             turn_fit(vb)
             turn_h(vb)

import math
from contextlib import ExitStack

import concourse.mybir as mybir
from concourse.masks import make_identity

K, T, S, D, N = 512, 2048, 1024, 4, 256
V = S // D
FLOPS = 2 * 2 * K * N * S

F32 = mybir.dt.float32
BF16 = mybir.dt.bfloat16
I32 = mybir.dt.int32
U32 = mybir.dt.uint32
U16 = mybir.dt.uint16
U8 = mybir.dt.uint8
FP8X4 = mybir.dt.float8_e4m3fn_x4
ACT = mybir.ActivationFunctionType
ALU = mybir.AluOpType

P = 128
PACK = 4
VB = V // P
MB = N // P
KNEE = 11.0
RATE, AMP = 0, 1
FIT_SCALE = 10.0 * D


def tile_picked_amp_p_kernel(tc, x_words, x_scales, w1, w2, te, sig, offs, out):
    nc = tc.nc
    with ExitStack() as ctx:
        keep = ctx.enter_context(tc.tile_pool(name="keep", bufs=1))
        psum = ctx.enter_context(tc.psum_pool(name="psum", bufs=1))

        def sb(name, shape, dtype=F32, tag=None):
            return keep.tile(shape, dtype, name=name, tag=tag or name, align_bytes=64)

        offsets = keep.tile([P, S // 16], U16, name="offsets")
        bank = [psum.tile([P, 512], F32, name="bank%d" % b) for b in range(8)]

        words_all = sb("words_all", [P, T], U32)
        scales_all = sb("scales_all", [P, T], U8)
        w_raw = [sb("w_raw%d" % i, [P, PACK, N]) for i in range(2)]
        t_col = sb("t_col", [P, VB, D])
        sig_sb = [sb("sig%d" % mb, [P, S]) for mb in range(MB)]

        nc.vector.memset(scales_all[:].bitcast(I32), 0)
        nc.sync.dma_start(offsets[:], offs)
        nc.sync.dma_start(out=words_all[:].bitcast(I32), in_=x_words[0].rearrange("p c r -> p (c r)").bitcast(I32))
        for q in range(4):
            nc.sync.dma_start(out=scales_all[32 * q : 32 * q + 4, :].bitcast(I32), in_=x_scales[0, 4 * q : 4 * q + 4, :].bitcast(I32))
        for i, w in enumerate((w2, w1)):
            nc.sync.dma_start(out=w_raw[i][:], in_=w.rearrange("(p j) n -> p j n", j=PACK))
        nc.sync.dma_start(out=t_col[:], in_=te[0, :].rearrange("(b v d) -> v b d", b=VB, d=D))
        for mb in range(MB):
            nc.sync.dma_start(out=sig_sb[mb][:], in_=sig[mb * P : (mb + 1) * P, :])

        knee = sb("knee", [P, 1])
        floor = sb("floor", [P, 1])
        nc.vector.memset(knee[:], KNEE)
        nc.scalar.activation(floor[:], knee[:], ACT.Sigmoid, scale=-1.0)
        ident = sb("ident", [P, P])
        make_identity(nc, ident[:])
        rate_scale = sb("rate_scale", [P, VB, D])
        nc.gpsimd.tensor_scalar(rate_scale[:], t_col[:], -1.0 / D, 0.0, ALU.mult, ALU.add)

        rate_bias = sb("rate_bias", [P, VB, D])
        nc.gpsimd.tensor_scalar(rate_bias[:], t_col[:], KNEE, 0.0, ALU.mult, ALU.add)

        t_sq = sb("t_sq", [P, VB, D])
        nc.gpsimd.tensor_tensor(t_sq[:], t_col[:], t_col[:], ALU.mult)

        w_codes = [sb("w_codes%d" % i, [P, N], U32) for i in range(2)]
        w_bytes = [sb("w_bytes%d" % i, [P, N], U8) for i in range(2)]
        x_codes, x_bytes = {}, {}

        def quantize(i):
            grouped = sb("w_grouped%d" % i, [P, N, PACK], BF16)
            nc.scalar.copy(grouped[:], w_raw[i][:].rearrange("p j n -> p n j"))
            nc.vector.quantize_mx(out=w_codes[i][:].bitcast(FP8X4), scales=w_bytes[i][:], in_=grouped[:].rearrange("p n j -> p (n j)"))

        def gather(table, vb, dst):
            picks = offsets[:, vb * P * D // 16 : (vb + 1) * P * D // 16]
            nc.vector.tensor_copy(dst[:].rearrange("p (d v) -> p v d", d=D), table[:].indirect(picks))

        x_codes[0] = sb("x_codes0", [P, D * P], U32)
        gather(words_all, 0, x_codes[0])
        x_bytes[0] = sb("x_bytes0", [P, D * P], U8)
        gather(scales_all, 0, x_bytes[0])
        x_codes[1] = sb("x_codes1", [P, D * P], U32)
        gather(words_all, 1, x_codes[1])
        quantize(RATE)
        x_bytes[1] = sb("x_bytes1", [P, D * P], U8, tag="w_grouped0")
        gather(scales_all, 1, x_bytes[1])
        quantize(AMP)

        def product(i, vb, d, dst):
            cols = slice(d * P, (d + 1) * P)
            nc.tensor.matmul_mx(
                out=dst,
                lhsT=x_codes[vb][:, cols].bitcast(FP8X4),
                lhsT_scale=x_bytes[vb][:, cols],
                rhs=w_codes[i][:].bitcast(FP8X4),
                rhs_scale=w_bytes[i][:],
                start=True,
                stop=True,
            )

        def rate_y(vb, d):
            return bank[2 * vb + d // 2][:, (d % 2) * N : (d % 2 + 1) * N]

        for vb in range(VB):
            for d in range(D):
                product(RATE, vb, d, rate_y(vb, d))
        for d in range(D):
            for vb in range(VB):
                product(AMP, vb, d, bank[D + d][:, vb * N : (vb + 1) * N])

        sigm_rate = sb("sigm_rate", [P, D, 2 * N], tag="w_raw1")
        sigm = [[sigm_rate[:, b, :] for b in range(D)], [sb("sigm_amp%d" % b, [P, 2 * N])[:] for b in range(D)]]
        prod_last = sb("prod_last", [P, 2, VB * N], tag="dec0")
        prod = [[sb("prod%d_%d" % (i, d), [P, VB * N]) for d in range(D - 1)] + [prod_last[:, 1 - i, :]] for i in range(2)]
        over = [[sb("over%d_%d" % (i, d), [P, VB * N]) for d in range(D)] for i in range(2)]
        log_prod = [sigm[AMP][0], sb("log_prod_amp", [P, VB * N])]
        amp4 = over[AMP][D - 1]
        rate4 = sb("rate4", [P, VB * N])
        over[RATE][D - 1] = rate4
        rate_over0 = sb("rate_over0", [P, N])
        amp_sq = sb("amp_sq", [P, VB * N])
        amp_quad = sb("amp_quad", [P, VB * N])
        damp = rate4

        blocks = [slice(vb * N, (vb + 1) * N) for vb in range(VB)]
        whole = slice(0, VB * N)

        def prod_step(i, d, cols, s):
            if d == 0:
                nc.vector.tensor_scalar(prod[i][0][:, cols], s, floor[:], None, ALU.max)
            else:
                nc.vector.scalar_tensor_tensor(prod[i][d][:, cols], s, floor[:], prod[i][d - 1][:, cols], ALU.max, ALU.mult)

        def over_step(i, d, cols, y, seed=None):
            if d > 0:
                nc.vector.scalar_tensor_tensor(over[i][d][:, cols], y, KNEE, over[i][d - 1][:, cols], ALU.max, ALU.add)
            elif seed is None:
                nc.vector.tensor_scalar(over[i][0][:, cols], y, KNEE, None, ALU.max)
            else:
                nc.vector.scalar_tensor_tensor(over[i][0][:, cols], y, KNEE, seed[:, cols], ALU.max, ALU.subtract)

        for i in range(2):
            for b in range(D):
                nc.scalar.activation(sigm[i][b], bank[D * i + b][:], ACT.Sigmoid, scale=-1.0)

        def rate_prod(vb, d):
            prod_step(RATE, d, blocks[vb], sigm[RATE][2 * vb + d // 2][:, (d % 2) * N : (d % 2 + 1) * N])

        def rate_over(vb, d):
            if (vb, d) == (0, D - 1):
                nc.vector.scalar_tensor_tensor(rate_over0[:], rate_y(0, d), KNEE, over[RATE][d - 1][:, blocks[0]], ALU.max, ALU.add)
            else:
                over_step(RATE, d, blocks[vb], rate_y(vb, d), log_prod[RATE] if vb else None)

        def rate_log(vb):
            nc.scalar.activation(log_prod[RATE][:, blocks[vb]], prod[RATE][D - 1][:, blocks[vb]], ACT.Ln)

        def rate_total(vb):
            nc.vector.tensor_tensor(rate4[:, blocks[vb]], rate_over0[:], log_prod[RATE][:, blocks[vb]], ALU.subtract)

        for d in range(D):
            rate_prod(0, d)
            rate_over(0, d)
        for d in range(D):
            rate_prod(1, d)
            prod_step(AMP, d, whole, sigm[AMP][d])
            if d == 0:
                rate_log(0)
                rate_total(0)
        rate_log(1)
        nc.scalar.activation(log_prod[AMP][:], prod[AMP][D - 1][:], ACT.Ln)
        for d in range(D):
            rate_over(1, d)
            over_step(AMP, d, whole, bank[D + d][:], log_prod[AMP])

        for vb in range(VB):
            for d in range(D):
                for mb in range(MB):
                    c0 = (d % 2) * N + mb * P
                    j0 = vb * P * D + d
                    nc.tensor.transpose(bank[2 * vb + d // 2][:, c0 : c0 + P], sig_sb[mb][:, j0 : (vb + 1) * P * D : D], ident[:])

        def turn(dst, col0, srcs):
            for n, src in enumerate(srcs):
                for mb in range(MB):
                    nc.tensor.matmul(
                        dst[:, col0 + mb * P : col0 + (mb + 1) * P],
                        src(mb),
                        ident[:],
                        start=(n == 0 and mb == 0),
                        stop=(n == len(srcs) - 1 and mb == MB - 1),
                        is_transpose=True,
                    )

        def cols_of(ap):
            return lambda mb: ap[:, mb * P : (mb + 1) * P]

        q_bank = [bank[4], bank[6]]
        h_bank = [bank[5], bank[7]]
        p_bank = [bank[0], bank[2]]
        u_bank = [bank[1], bank[3]]

        def per_block(name, shape):
            return [sb("%s%d" % (name, vb), shape) for vb in range(VB)]

        dec = per_block("dec", [P, D, N])
        dec_sq = per_block("dec_sq", [P, D, N])
        dec_sig = per_block("dec_sig", [P, D, N])
        slope_sq = per_block("slope_sq", [P, D, N])
        q1 = per_block("q1_", [P, D, N])
        p1 = per_block("p1_", [P, D, N])
        q1_sq = per_block("q1_sq", [P, N])
        q1_p1 = per_block("q1_p1", [P, N])
        hrr = per_block("hrr", [P, N])
        det_lead = per_block("det_lead", [P, N])
        det = per_block("det", [P, N])
        num_lead = per_block("num_lead", [P, N])
        num = per_block("num", [P, N])
        root = per_block("root", [P, N])
        inv = per_block("inv", [P, N])
        res = per_block("res", [P, N])

        def decays(vb):
            for d in range(D):
                nc.scalar.activation(dec[vb][:, d, :], rate4[:, blocks[vb]], ACT.Exp, scale=rate_scale[:, vb, d : d + 1], bias=rate_bias[:, vb, d : d + 1])

        def squares(vb, halves=(0, 1)):
            for h in halves:
                nc.scalar.activation(dec_sq[vb][:, 2 * h : 2 * h + 2, :], dec[vb][:, 2 * h : 2 * h + 2, :], ACT.Square)

        def slopes(vb):
            for d in range(0 if vb in (1,) else D):
                nc.scalar.activation(slope_sq[vb][:, d, :], dec[vb][:, d, :], ACT.Square, scale=t_col[:, vb, d : d + 1])

        def timed_step(acc, src, vb, d, col=t_col):
            t_d = col[:, vb, d : d + 1]
            if d == 0:
                nc.vector.tensor_scalar(acc[:, 0, :], src[:, 0, :], t_d, None, ALU.mult)
            else:
                nc.vector.scalar_tensor_tensor(acc[:, d, :], src[:, d, :], t_d, acc[:, d - 1, :], ALU.mult, ALU.add)

        def weigh(vb, h):
            nc.vector.scalar_tensor_tensor(
                dec_sig[vb][:, 2 * h : 2 * h + 2, :],
                dec[vb][:, 2 * h : 2 * h + 2, :],
                FIT_SCALE,
                bank[2 * vb + h][:].rearrange("p (d m) -> p d m", d=2),
                ALU.mult,
                ALU.mult,
            )

        def turn_fit(vb):
            pairs = sb("pairs%d" % vb, [P, 2, N])
            if vb in (1,):
                nc.vector.tensor_tensor(pairs[:], dec_sig[vb][:, 0:2, :], dec_sig[vb][:, 2:4, :], ALU.add)
            turn(p_bank[vb], 0, [cols_of((pairs if vb in (1,) else dec_sig[vb])[:, d, :]) for d in range(2 if vb in (1,) else D)] + [cols_of(amp4[:, blocks[vb]])])

        def turn_q0(vb):
            turn(q_bank[vb], 0, [cols_of(dec_sq[vb][:, d, :]) for d in range(D)])

        def turn_h(vb):
            turn(h_bank[vb], 0, [cols_of(slope_sq[vb][:, d, :]) for d in range(D - 1 if vb in (1,) else 0, D)] + [cols_of(damp[:, blocks[vb]])])
            nc.scalar.copy(hrr[vb][:], h_bank[vb][:, 0:N])

        def cross(vb):
            nc.scalar.activation(q1_sq[vb][:], q1[vb][:, D - 1, :], ACT.Square)
            nc.vector.tensor_tensor(q1_p1[vb][:], q1[vb][:, D - 1, :], p1[vb][:, D - 1, :], ALU.mult)
            turn(q_bank[vb], N, [cols_of(q1_sq[vb][:])])
            turn(u_bank[vb], 0, [cols_of(q1_p1[vb][:])])

        def det_first(vb):
            nc.vector.scalar_tensor_tensor(det_lead[vb][:], q_bank[vb][:, 0:N], 0.1, hrr[vb][:], ALU.add, ALU.mult)

        def num_first(vb):
            nc.vector.scalar_tensor_tensor(num_lead[vb][:], p_bank[vb][:, 0:N], D * (0.3 - KNEE), hrr[vb][:], ALU.add, ALU.mult)

        def det_second(vb):
            nc.vector.tensor_tensor(det[vb][:], det_lead[vb][:], q_bank[vb][:, N : 2 * N], ALU.subtract)
            nc.scalar.activation(root[vb][:], det[vb][:], ACT.Abs_reciprocal_sqrt)
            nc.scalar.activation(inv[vb][:], root[vb][:], ACT.Square)

        def num_second(vb):
            nc.vector.tensor_tensor(num[vb][:], num_lead[vb][:], u_bank[vb][:, 0:N], ALU.subtract)

        def finish(vb):
            nc.vector.scalar_tensor_tensor(res[vb][:], num[vb][:], 1.0 / FIT_SCALE, inv[vb][:], ALU.mult, ALU.mult)
            nc.sync.dma_start(
                out=out.rearrange("(b p) v -> p b v", p=P)[:, :, vb * P : (vb + 1) * P],
                in_=res[vb][:].rearrange("p (b v) -> p b v", b=MB),
            )

        decays(0)
        for h in range(2):
            pair = dec[0][:, 2 * h : 2 * h + 2, :]
            nc.gpsimd.tensor_tensor(dec_sq[0][:, 2 * h : 2 * h + 2, :], pair, pair, ALU.mult)
        decays(1)
        squares(1)
        nc.scalar.activation(amp_sq[:], amp4[:], ACT.Square, scale=1.0 / D, bias=0.3 - KNEE)
        nc.scalar.activation(amp_quad[:], amp_sq[:], ACT.Square)
        nc.scalar.activation(damp[:], amp_quad[:], ACT.Abs_reciprocal_sqrt, scale=1.0 / (0.3 * 0.3))
        slopes(0)
        slopes(1)
        for vb in range(VB):
            weigh(vb, 0)
            weigh(vb, 1)
            for d in range(D):
                timed_step(p1[vb], dec_sig[vb], vb, d)
                timed_step(q1[vb], dec_sq[vb], vb, d)
                if vb in (1,):
                    timed_step(slope_sq[vb], dec_sq[vb], vb, d, t_sq)
            turn_q0(vb)
            turn_fit(vb)
            turn_h(vb)
            cross(vb)
        for step in (det_first, det_second, num_first, num_second, finish):
            for vb in range(VB):
                step(vb)
